import numpy as np
import ml_dtypes


def mxq(x, axis, fmt="e4m3"):
    dtype, down = {"e4m3": (ml_dtypes.float8_e4m3fn, 7), "e5m2": (ml_dtypes.float8_e5m2, 14)}[fmt]
    v = np.moveaxis(np.asarray(x, np.float32).astype(ml_dtypes.bfloat16).astype(np.float64), axis, -1)
    blocks = v.reshape(v.shape[:-1] + (-1, 32))
    amax = np.abs(blocks).max(-1, keepdims=True)
    byte = np.maximum(np.where(amax > 0, np.frexp(amax)[1] - 1 + 127, 0) - down, 1)
    scale = np.exp2(byte - 127.0)
    codes = (blocks / scale).astype(np.float32).astype(dtype).astype(np.float64)
    return np.moveaxis((codes * scale).reshape(v.shape), -1, axis)


WIDE = False


def mx_kscale(k):
    if not WIDE:
        return np.ones(k)
    levels = np.array([10, -10, 5, -5, 0])
    if k % 512:
        return np.exp2(np.random.permutation(np.resize(levels, k // 32))).repeat(32)
    a = np.empty((k // 512, 16))
    for p in range(k // 512):
        a[p, :8] = np.random.permutation(np.resize(levels, 8))
        for g in range(8):
            far = levels[np.abs(levels - a[p, g]) >= 10]
            a[p, g + 8] = far[np.random.randint(len(far))]
    return np.exp2(a.ravel()).repeat(32)


def f64(x):
    return np.asarray(x).astype(np.float64)


def striped(idx):
    return np.tile(idx.reshape(-1, 16).T, (8, 1)).astype(np.uint16)


def unstriped(offs):
    return offs[:16].T.reshape(-1).astype(np.int64)


def silu(v):
    return v / (1.0 + np.exp(-np.maximum(v, -700.0)))


def d_silu(v):
    s = 1.0 / (1.0 + np.exp(-np.maximum(v, -700.0)))
    return s * (1.0 + v * (1.0 - s))


K, T, E, C, H, N = 384, 512, 4, 256, 512, 1536


def by_expert(wq, xq):
    return np.concatenate([wq[e].T @ xq[:, e * C:(e + 1) * C] for e in range(E)], axis=1)


def setup_inputs():
    n = np.random.standard_normal
    s = mx_kscale(N)[:, None]
    u = mx_kscale(H)
    first = np.random.permutation(np.repeat(np.arange(E), T // E))
    second = (first + 1 + np.random.permutation(np.repeat(np.arange(E - 1), -(-T // (E - 1)))[:T])) % E
    while np.bincount(second, minlength=E).max() != T // E:
        load = np.bincount(second, minlength=E); hi, lo = int(load.argmax()), int(load.argmin())
        t = np.flatnonzero((second == hi) & (first != lo))[0]; second[t] = lo
    slot_token = np.empty(E * C, np.int64); pos = np.empty((2, T), np.int64); fill = np.zeros(E, np.int64)
    place = np.stack([np.random.permutation(C) for _ in range(E)])
    for r, deal in enumerate((first, second)):
        for t in np.random.permutation(T):
            e = deal[t]; j = e * C + place[e, fill[e]]; fill[e] += 1; slot_token[j] = t; pos[r, t] = j
    g = np.random.uniform(0.2, 0.8, T)
    w_slot = np.empty(E * C); w_slot[pos[0]] = g; w_slot[pos[1]] = 1.0 - g
    return {
        "dyT": (n((N, T)) * s).astype(np.float32),
        "a1": n((H, E * C)).astype(np.float32),
        "a3": n((H, E * C)).astype(np.float32),
        "w2": (n((E, N, H)) / np.sqrt(N) / s[None] * u[None, None, :]).astype(np.float32),
        "w1": (n((E, H, K)) / np.sqrt(H) / u[None, :, None]).astype(np.float32),
        "w3": (n((E, H, K)) / np.sqrt(H) / u[None, :, None]).astype(np.float32),
        "gate": np.tile(w_slot, (N, 1)).astype(np.float32),
        "offs": striped(slot_token),
        "pos1": striped(pos[0]),
        "pos2": striped(pos[1]),
    }


def reference(dyT, a1, a3, w2, w1, w3, gate, offs, pos1, pos2):
    idx = unstriped(offs)
    gq = mxq(f64(gate) * f64(dyT)[:, idx], 0, "e4m3")
    dh = by_expert(mxq(f64(w2), 1, "e4m3"), gq)
    da1 = dh * f64(a3) * d_silu(f64(a1))
    da3 = dh * silu(f64(a1))
    dx = by_expert(mxq(f64(w1), 1, "e4m3"), mxq(da1, 0, "e4m3")) + by_expert(mxq(f64(w3), 1, "e4m3"), mxq(da3, 0, "e4m3"))
    return dx[:, unstriped(pos1)] + dx[:, unstriped(pos2)]

@@ -1,0 +1,396 @@
+from contextlib import ExitStack
+
+import concourse.mybir as mybir
+
+N, T, E, C, H, K = 1536, 512, 4, 256, 512, 384
+S = E * C
+
+F32 = mybir.dt.float32
+BF16 = mybir.dt.bfloat16
+U32 = mybir.dt.uint32
+U16 = mybir.dt.uint16
+U8 = mybir.dt.uint8
+FP8X4 = mybir.dt.float8_e4m3fn_x4
+MULT = mybir.AluOpType.mult
+ADD = mybir.AluOpType.add
+SUB = mybir.AluOpType.subtract
+SILU = mybir.ActivationFunctionType.Silu
+SIGMOID = mybir.ActivationFunctionType.Sigmoid
+
+P = 128
+PAIR = 2 * C
+FILL = 32
+PASSES = N // 512
+MT = K // P
+G4B, W2B, W2Q, RAW = 2, 3, 5, 5
+
+FLOPS = 2 * S * H * N + 2 * 2 * S * H * K
+BYTES = 4 * (N * T + 2 * H * S + E * N * H + 2 * E * H * K + S + K * T) + 2 * 128 * (64 + 32 + 32)
+
+
+def tile_moe_bdx_glu_silu_kernel(
+    tc, dyT, a1, a3, w2, w1, w3, gate, offs, pos1, pos2, out
+):
+    nc = tc.nc
+
+    with ExitStack() as ctx:
+        lists = ctx.enter_context(tc.tile_pool(name="lists", bufs=1))
+        held = ctx.enter_context(tc.tile_pool(name="held", bufs=1))
+        ring = ctx.enter_context(tc.tile_pool(name="ring", bufs=2))
+        psum = ctx.enter_context(tc.psum_pool(name="psum", bufs=4))
+
+        offs_sb = lists.tile([P, S // 16], U16, name="offs_sb")
+        pos1_sb = lists.tile([P, T // 16], U16, name="pos1_sb")
+        pos2_sb = lists.tile([P, T // 16], U16, name="pos2_sb")
+
+        dy_rows = dyT.rearrange("(c p j) w -> c p (j w)", p=P, j=4)
+        a1_rows = a1.rearrange("(q t) n -> q t n", t=4)
+        a3_rows = a3.rearrange("(q t) n -> q t n", t=4)
+
+        dy, gates, a3s, g4s, gbs, w2b, w13b, zs, das, dhs = {}, {}, {}, {}, {}, {}, {}, {}, {}, {}
+        hid = held.tile([P, 4, S], F32, name="hid")
+        sig = held.tile([P, 4, S], F32, name="sig")
+        raw2, raw13, gq, w2q, w13q, daq = {}, {}, {}, {}, {}, {}
+        dxs = []
+        for m in range(MT):
+            dxs.append(held.tile([P, S], F32, name=f"dx_rows{m}"))
+
+        def load_gate(r):
+            gates[r] = held.tile([P, PAIR], F32, name=f"gate{r}")
+            nc.sync.dma_start(out=gates[r][:], in_=gate[0:P, r * PAIR : (r + 1) * PAIR])
+
+        def load_dy(c, j):
+            t = held.tile([P, T + FILL], F32, name=f"dy{c}_{j}")
+            dy[c, j] = t
+            if j < 3:
+                nc.sync.dma_start(out=t[:], in_=dy_rows[c, :, j * T : (j + 1) * T + FILL])
+            else:
+                nc.sync.dma_start(out=t[:, 0:T], in_=dy_rows[c, :, j * T : (j + 1) * T])
+                nc.sync.dma_start(out=t[:, T : T + FILL], in_=dy_rows[c, :, 0:FILL])
+
+        def load_a1(t):
+            nc.sync.dma_start(out=hid[:, t, :], in_=a1_rows[:, t, :])
+
+        def load_a3(r):
+            a3s[r] = ring.tile([P, 4, PAIR], F32, name="a3_sb", bufs=1)
+            nc.sync.dma_start(out=a3s[r][:], in_=a3_rows[:, :, r * PAIR : (r + 1) * PAIR])
+
+        def load_w2(e, c):
+            raw2[e, c] = ring.tile([P, 4, H], F32, name="w_raw", bufs=RAW)
+            nc.sync.dma_start(
+                out=raw2[e, c][:],
+                in_=w2[e, c * 512 : (c + 1) * 512, :].rearrange("(p j) w -> p j w", j=4),
+            )
+
+        def load_w13(e):
+            for k, w in ((0, w1), (1, w3)):
+                raw13[e, k] = ring.tile([P, 4, K], F32, name="w_raw", bufs=RAW)
+                nc.sync.dma_start(
+                    out=raw13[e, k][:], in_=w[e, :, :].rearrange("(p j) w -> p j w", j=4)
+                )
+
+        def load_pos():
+            nc.sync.dma_start(pos1_sb[:], pos1)
+            nc.sync.dma_start(pos2_sb[:], pos2)
+
+        def half(r):
+            return slice(r * PAIR, (r + 1) * PAIR)
+
+        def sigmoid(t):
+            nc.scalar.activation(out=sig[:, t, :], in_=hid[:, t, :], func=SIGMOID)
+
+        def silu_neg(r):
+            zs[r] = ring.tile([P, 4, PAIR], F32, name="z", bufs=1)
+            nc.scalar.activation(out=zs[r][:], in_=hid[:, :, half(r)], func=SILU, scale=-1.0)
+
+        def silu_pos(r):
+            nc.scalar.activation(out=hid[:, :, half(r)], in_=hid[:, :, half(r)], func=SILU)
+
+        def slope1(r):
+            nc.vector.scalar_tensor_tensor(
+                out=sig[:, :, half(r)], in0=zs[r][:], scalar=1.0, in1=sig[:, :, half(r)], op0=SUB, op1=MULT
+            )
+
+        def slope2(r):
+            nc.vector.scalar_tensor_tensor(
+                out=sig[:, :, half(r)], in0=sig[:, :, half(r)], scalar=-1.0, in1=a3s[r][:], op0=MULT, op1=MULT
+            )
+
+        def gather(r, c):
+            g4 = ring.tile([P, 4, PAIR], F32, name="g4", bufs=G4B)
+            g4s[r, c] = g4
+            for j in range(4):
+                nc.vector.tensor_tensor(
+                    g4[:, j, :],
+                    dy[c, j][:].indirect(offs_sb[:, r * PAIR // 16 : (r + 1) * PAIR // 16]),
+                    gates[r][:],
+                    MULT,
+                )
+
+        def interleave(engine, dst, src):
+            dst = dst.rearrange("p (c i) t -> p c t i", i=4)
+            src = src.rearrange("p t (c i) -> p c t i", i=4)
+            if engine == "S":
+                nc.scalar.copy(out=dst, in_=src)
+            else:
+                nc.vector.tensor_copy(out=dst, in_=src)
+
+        def cast_g(r, c, engine="S"):
+            gb = ring.tile([P, PAIR, 4], BF16, name="gb", bufs=2, align_bytes=64)
+            gbs[r, c] = gb
+            interleave(engine, gb[:], g4s[r, c][:])
+
+        def quant_g(r, c):
+            q = ring.tile([P, PAIR], U32, name="gq", bufs=5, align_bytes=64)
+            s = ring.tile([P, PAIR], U8, name="gs", bufs=5, align_bytes=64)
+            nc.vector.quantize_mx(
+                out=q[:].bitcast(FP8X4), scales=s[:], in_=gbs[r, c][:].rearrange("p w j -> p (w j)")
+            )
+            gq[r, c] = (q, s)
+
+        def cast_w2(e, c, engine="S"):
+            wb = ring.tile([P, H * 4], BF16, name="w2b", bufs=W2B, align_bytes=64)
+            w2b[e, c] = wb
+            dst = wb[:].rearrange("p (t m j) -> p m j t", t=4, j=4)
+            src = raw2[e, c][:].rearrange("p j (m t) -> p m j t", t=4)
+            if engine == "S":
+                nc.scalar.copy(out=dst, in_=src)
+            else:
+                nc.vector.tensor_copy(out=dst, in_=src)
+
+        def quant_w2(e, c):
+            q = ring.tile([P, H], U32, name="w2q", bufs=W2Q, align_bytes=64)
+            s = ring.tile([P, H], U8, name="w2s", bufs=W2Q, align_bytes=64)
+            nc.vector.quantize_mx(out=q[:].bitcast(FP8X4), scales=s[:], in_=w2b[e, c][:])
+            w2q[e, c] = (q, s)
+
+        def cast_w13(e, m, engines="SS"):
+            wb = ring.tile([P, 2, P, 4], BF16, name="w13b", bufs=3, align_bytes=64)
+            w13b[e, m] = wb
+            for k in range(2):
+                interleave(engines[k], wb[:, k], raw13[e, k][:, :, m * P : (m + 1) * P])
+
+        def quant_w13(e, m):
+            q = ring.tile([P, 2 * P], U32, name="w13q", bufs=6, align_bytes=64)
+            s = ring.tile([P, 2 * P], U8, name="w13s", bufs=6, align_bytes=64)
+            nc.vector.quantize_mx(
+                out=q[:].bitcast(FP8X4), scales=s[:], in_=w13b[e, m][:].rearrange("p k w j -> p (k w j)")
+            )
+            w13q[e, m] = (q, s)
+
+        def first(e, half):
+            r = e // 2
+            if half == 0:
+                das[e] = ring.tile([P, 2, C, 4], BF16, name="da", bufs=2, align_bytes=64)
+            da = das[e]
+            dh = psum.tile([P, 4, P], F32, name="dh")
+            col = (e % 2) * C + half * P
+            for t in range(4):
+                for c in range(PASSES):
+                    wq, ws = w2q[e, c]
+                    q, s = gq[r, c]
+                    nc.tensor.matmul_mx(
+                        out=dh[:, t, :],
+                        lhsT=wq[:, t * P : (t + 1) * P].bitcast(FP8X4),
+                        lhsT_scale=ws[:, t * P : (t + 1) * P],
+                        rhs=q[:, col : col + P].bitcast(FP8X4),
+                        rhs_scale=s[:, col : col + P],
+                        start=(c == 0),
+                        stop=(c == PASSES - 1),
+                    )
+            dhs[e, half] = dh
+
+        def times(e, half):
+            da, dh = das[e], dhs[e, half]
+            slot = e * C + half * P
+            for k, factor in ((0, sig), (1, hid)):
+                nc.vector.tensor_tensor(
+                    da[:, k, half * P : (half + 1) * P].rearrange("p (c i) t -> p c t i", i=4),
+                    dh[:].rearrange("p t (c i) -> p c t i", i=4),
+                    factor[:, :, slot : slot + P].rearrange("p t (c i) -> p c t i", i=4),
+                    MULT,
+                )
+
+        def quant_da(e):
+            q = ring.tile([P, 2 * C], U32, name="daq", bufs=3, align_bytes=64)
+            s = ring.tile([P, 2 * C], U8, name="das", bufs=3, align_bytes=64)
+            nc.vector.quantize_mx(
+                out=q[:].bitcast(FP8X4), scales=s[:], in_=das[e][:].rearrange("p k w j -> p (k w j)")
+            )
+            daq[e] = (q, s)
+
+        def second_product(e, m):
+            wq, ws = w13q[e, m]
+            q, s = daq[e]
+            dx = psum.tile([P, C], F32, name="dx")
+            for k in range(2):
+                nc.tensor.matmul_mx(
+                    out=dx[:],
+                    lhsT=wq[:, k * P : (k + 1) * P].bitcast(FP8X4),
+                    lhsT_scale=ws[:, k * P : (k + 1) * P],
+                    rhs=q[:, k * C : (k + 1) * C].bitcast(FP8X4),
+                    rhs_scale=s[:, k * C : (k + 1) * C],
+                    start=(k == 0),
+                    stop=(k == 1),
+                )
+            nc.scalar.copy(out=dxs[m][:, e * C : (e + 1) * C], in_=dx[:])
+
+        def combine(m):
+            first = ring.tile([P, T], F32, name="first", bufs=2)
+            second = ring.tile([P, T], F32, name="second", bufs=2)
+            nc.vector.tensor_copy(first[:], dxs[m][:].indirect(pos1_sb[:]))
+            nc.vector.tensor_copy(second[:], dxs[m][:].indirect(pos2_sb[:]))
+            nc.vector.tensor_tensor(first[:], first[:], second[:], ADD)
+            nc.sync.dma_start(out=out[m * P : (m + 1) * P, :], in_=first[:])
+
+        nc.sync.dma_start(offs_sb[:], offs)
+        load_gate(0)
+        load_dy(0,0)
+        load_dy(0,1)
+        load_a1(0)
+        load_dy(0,2)
+        load_dy(0,3)
+        load_w2(0,0)
+        load_a1(1)
+        load_dy(1,0)
+        load_dy(1,1)
+        load_a1(2)
+        load_dy(1,2)
+        load_dy(1,3)
+        load_w2(0,1)
+        load_dy(2,0)
+        load_dy(2,1)
+        load_a1(3)
+        load_dy(2,2)
+        load_dy(2,3)
+        load_w2(0,2)
+        load_a3(0)
+        load_gate(1)
+        load_w2(1,0)
+        load_w2(1,1)
+        gather(0,0)
+        cast_g(0,0)
+        sigmoid(0)
+        cast_w2(0,0)
+        load_w2(1,2)
+        quant_g(0,0)
+        quant_w2(0,0)
+        gather(0,1)
+        cast_g(0,1,'V')
+        sigmoid(1)
+        cast_w2(0,1)
+        quant_g(0,1)
+        quant_w2(0,1)
+        gather(0,2)
+        cast_g(0,2)
+        sigmoid(2)
+        sigmoid(3)
+        cast_w2(0,2)
+        load_w13(0)
+        load_pos()
+        quant_g(0,2)
+        quant_w2(0,2)
+        silu_neg(0)
+        slope1(0)
+        silu_pos(0)
+        slope2(0)
+        first(0,0)
+        first(0,1)
+        cast_w2(1,0,'V')
+        load_w2(2,0)
+        cast_w2(1,1)
+        cast_w2(1,2)
+        load_w13(1)
+        load_a3(1)
+        silu_neg(1)
+        slope1(1)
+        gather(1,0)
+        times(0,0)
+        times(0,1)
+        quant_da(0)
+        quant_w2(1,0)
+        quant_w2(1,1)
+        quant_w2(1,2)
+        first(1,0)
+        first(1,1)
+        cast_w13(0,0)
+        quant_w13(0,0)
+        cast_w13(0,1)
+        quant_w13(0,1)
+        cast_w13(0,2)
+        load_w2(2,1)
+        load_w2(2,2)
+        quant_w13(0,2)
+        cast_g(1,0)
+        gather(1,1)
+        times(1,0)
+        times(1,1)
+        quant_da(1)
+        second_product(0,0)
+        second_product(0,1)
+        second_product(0,2)
+        cast_w2(2,0,'V')
+        load_w2(3,0)
+        quant_g(1,0)
+        cast_g(1,1)
+        gather(1,2)
+        cast_w13(1,0)
+        quant_w13(1,0)
+        cast_w13(1,1)
+        quant_w13(1,1)
+        cast_w13(1,2)
+        load_w2(3,1)
+        load_w2(3,2)
+        quant_w13(1,2)
+        cast_w2(2,1)
+        quant_g(1,1)
+        cast_w2(2,2)
+        load_w13(2)
+        cast_g(1,2)
+        second_product(1,0)
+        second_product(1,1)
+        second_product(1,2)
+        silu_pos(1)
+        slope2(1)
+        quant_w2(2,0)
+        quant_w2(2,1)
+        quant_w2(2,2)
+        quant_g(1,2)
+        first(2,0)
+        first(2,1)
+        cast_w2(3,0,'V')
+        cast_w2(3,1)
+        load_w13(3)
+        cast_w2(3,2)
+        times(2,0)
+        times(2,1)
+        quant_da(2)
+        quant_w2(3,0)
+        quant_w2(3,1)
+        quant_w2(3,2)
+        first(3,0)
+        first(3,1)
+        cast_w13(2,0)
+        cast_w13(3,0)
+        quant_w13(2,0)
+        quant_w13(3,0)
+        times(3,0)
+        times(3,1)
+        quant_da(3)
+        cast_w13(2,1)
+        cast_w13(3,1)
+        second_product(2,0)
+        second_product(3,0)
+        quant_w13(2,1)
+        quant_w13(3,1)
+        cast_w13(2,2)
+        cast_w13(3,2)
+        combine(0)
+        second_product(2,1)
+        second_product(3,1)
+        quant_w13(2,2)
+        quant_w13(3,2)
+        second_product(2,2)
+        second_product(3,2)
+        combine(1)
+        combine(2)

@@ -22,7 +22,7 @@ PAIR = 2 * C
 FILL = 32
 PASSES = N // 512
 MT = K // P
-G4B, W2B, W2Q, RAW = 2, 3, 5, 5
+G4B, W2B, W2Q, RAW = 3, 3, 4, 6
 
 FLOPS = 2 * S * H * N + 2 * 2 * S * H * K
 BYTES = 4 * (N * T + 2 * H * S + E * N * H + 2 * E * H * K + S + K * T) + 2 * 128 * (64 + 32 + 32)
@@ -100,7 +100,7 @@ def tile_moe_bdx_glu_silu_kernel(
             nc.scalar.activation(out=sig[:, t, :], in_=hid[:, t, :], func=SIGMOID)
 
         def silu_neg(r):
-            zs[r] = ring.tile([P, 4, PAIR], F32, name="z", bufs=1)
+            zs[r] = ring.tile([P, 4, PAIR], F32, name="f32", bufs=G4B)
             nc.scalar.activation(out=zs[r][:], in_=hid[:, :, half(r)], func=SILU, scale=-1.0)
 
         def silu_pos(r):
@@ -117,7 +117,7 @@ def tile_moe_bdx_glu_silu_kernel(
             )
 
         def gather(r, c):
-            g4 = ring.tile([P, 4, PAIR], F32, name="g4", bufs=G4B)
+            g4 = ring.tile([P, 4, PAIR], F32, name="f32", bufs=G4B)
             g4s[r, c] = g4
             for j in range(4):
                 nc.vector.tensor_tensor(
@@ -164,19 +164,19 @@ def tile_moe_bdx_glu_silu_kernel(
             nc.vector.quantize_mx(out=q[:].bitcast(FP8X4), scales=s[:], in_=w2b[e, c][:])
             w2q[e, c] = (q, s)
 
-        def cast_w13(e, m, engines="SS"):
-            wb = ring.tile([P, 2, P, 4], BF16, name="w13b", bufs=3, align_bytes=64)
-            w13b[e, m] = wb
-            for k in range(2):
-                interleave(engines[k], wb[:, k], raw13[e, k][:, :, m * P : (m + 1) * P])
+        def cast_w13(r, m, engines="SSSS"):
+            wb = ring.tile([P, 4, P, 4], BF16, name="w13b", bufs=2, align_bytes=64)
+            w13b[r, m] = wb
+            for i in range(4):
+                interleave(engines[i], wb[:, i], raw13[2 * r + i // 2, i % 2][:, :, m * P : (m + 1) * P])
 
-        def quant_w13(e, m):
-            q = ring.tile([P, 2 * P], U32, name="w13q", bufs=6, align_bytes=64)
-            s = ring.tile([P, 2 * P], U8, name="w13s", bufs=6, align_bytes=64)
+        def quant_w13(r, m):
+            q = ring.tile([P, 4 * P], U32, name="w13q", bufs=3, align_bytes=64)
+            s = ring.tile([P, 4 * P], U8, name="w13s", bufs=3, align_bytes=64)
             nc.vector.quantize_mx(
-                out=q[:].bitcast(FP8X4), scales=s[:], in_=w13b[e, m][:].rearrange("p k w j -> p (k w j)")
+                out=q[:].bitcast(FP8X4), scales=s[:], in_=w13b[r, m][:].rearrange("p k w j -> p (k w j)")
             )
-            w13q[e, m] = (q, s)
+            w13q[r, m] = (q, s)
 
         def first(e, half):
             r = e // 2
@@ -219,178 +219,162 @@ def tile_moe_bdx_glu_silu_kernel(
             )
             daq[e] = (q, s)
 
-        def second_product(e, m):
-            wq, ws = w13q[e, m]
-            q, s = daq[e]
-            dx = psum.tile([P, C], F32, name="dx")
-            for k in range(2):
-                nc.tensor.matmul_mx(
-                    out=dx[:],
-                    lhsT=wq[:, k * P : (k + 1) * P].bitcast(FP8X4),
-                    lhsT_scale=ws[:, k * P : (k + 1) * P],
-                    rhs=q[:, k * C : (k + 1) * C].bitcast(FP8X4),
-                    rhs_scale=s[:, k * C : (k + 1) * C],
-                    start=(k == 0),
-                    stop=(k == 1),
-                )
-            nc.scalar.copy(out=dxs[m][:, e * C : (e + 1) * C], in_=dx[:])
+        def second(r, m):
+            wq, ws = w13q[r, m]
+            dx = psum.tile([P, 2, C], F32, name="dx")
+            for i in range(2):
+                q, s = daq[2 * r + i]
+                for k in range(2):
+                    w = slice((2 * i + k) * P, (2 * i + k + 1) * P)
+                    nc.tensor.matmul_mx(
+                        out=dx[:, i, :],
+                        lhsT=wq[:, w].bitcast(FP8X4),
+                        lhsT_scale=ws[:, w],
+                        rhs=q[:, k * C : (k + 1) * C].bitcast(FP8X4),
+                        rhs_scale=s[:, k * C : (k + 1) * C],
+                        start=(k == 0),
+                        stop=(k == 1),
+                    )
+            nc.scalar.copy(out=dxs[m][:, half(r)], in_=dx[:].rearrange("p i n -> p (i n)"))
 
-        def combine(m):
-            first = ring.tile([P, T], F32, name="first", bufs=2)
-            second = ring.tile([P, T], F32, name="second", bufs=2)
-            nc.vector.tensor_copy(first[:], dxs[m][:].indirect(pos1_sb[:]))
-            nc.vector.tensor_copy(second[:], dxs[m][:].indirect(pos2_sb[:]))
-            nc.vector.tensor_tensor(first[:], first[:], second[:], ADD)
-            nc.sync.dma_start(out=out[m * P : (m + 1) * P, :], in_=first[:])
+        def combine(m, engine="V"):
+            both = ring.tile([P, 2, T], F32, name="f32", bufs=G4B)
+            nc.vector.tensor_copy(both[:, 0, :], dxs[m][:].indirect(pos1_sb[:]))
+            nc.vector.tensor_copy(both[:, 1, :], dxs[m][:].indirect(pos2_sb[:]))
+            adder = nc.vector if engine == "V" else nc.gpsimd
+            adder.tensor_tensor(both[:, 0, :], both[:, 0, :], both[:, 1, :], ADD)
+            nc.sync.dma_start(out=out[m * P : (m + 1) * P, :], in_=both[:, 0, :])
 
         nc.sync.dma_start(offs_sb[:], offs)
-        load_gate(0)
         load_dy(0,0)
+        load_gate(0)
         load_dy(0,1)
+        load_pos()
         load_a1(0)
         load_dy(0,2)
         load_dy(0,3)
-        load_w2(0,0)
-        load_a1(1)
         load_dy(1,0)
+        load_a1(1)
         load_dy(1,1)
-        load_a1(2)
         load_dy(1,2)
+        load_w2(0,0)
         load_dy(1,3)
-        load_w2(0,1)
         load_dy(2,0)
         load_dy(2,1)
-        load_a1(3)
         load_dy(2,2)
+        load_w2(0,1)
         load_dy(2,3)
-        load_w2(0,2)
-        load_a3(0)
+        load_a1(2)
+        load_a1(3)
         load_gate(1)
+        load_w2(0,2)
         load_w2(1,0)
         load_w2(1,1)
-        gather(0,0)
-        cast_g(0,0)
-        sigmoid(0)
-        cast_w2(0,0)
         load_w2(1,2)
-        quant_g(0,0)
-        quant_w2(0,0)
+        gather(0,0)
+        sigmoid(0)
         gather(0,1)
-        cast_g(0,1,'V')
         sigmoid(1)
+        cast_g(0,0)
+        quant_g(0,0)
+        cast_w2(0,0)
+        cast_g(0,1)
         cast_w2(0,1)
-        quant_g(0,1)
-        quant_w2(0,1)
-        gather(0,2)
-        cast_g(0,2)
+        load_w13(0)
+        load_a3(0)
         sigmoid(2)
         sigmoid(3)
-        cast_w2(0,2)
-        load_w13(0)
-        load_pos()
-        quant_g(0,2)
-        quant_w2(0,2)
+        gather(0,2)
+        cast_g(0,2)
+        quant_w2(0,0)
+        quant_w2(0,1)
+        gather(1,0)
+        cast_w2(0,2,'V')
+        gather(1,1)
+        quant_g(0,1)
         silu_neg(0)
         slope1(0)
+        quant_w2(0,2)
+        cast_w2(1,0)
+        load_w13(1)
         silu_pos(0)
-        slope2(0)
+        quant_g(0,2)
         first(0,0)
         first(0,1)
-        cast_w2(1,0,'V')
-        load_w2(2,0)
+        slope2(0)
         cast_w2(1,1)
-        cast_w2(1,2)
-        load_w13(1)
-        load_a3(1)
-        silu_neg(1)
-        slope1(1)
-        gather(1,0)
+        load_w2(2,0)
+        cast_g(1,0)
+        cast_w2(1,2,'V')
+        load_w2(2,1)
+        cast_w13(0,0,'SSSV')
+        cast_g(1,1,'V')
         times(0,0)
-        times(0,1)
-        quant_da(0)
         quant_w2(1,0)
         quant_w2(1,1)
+        times(0,1)
+        quant_w13(0,0)
+        quant_g(1,0)
+        silu_neg(1)
         quant_w2(1,2)
         first(1,0)
-        first(1,1)
-        cast_w13(0,0)
-        quant_w13(0,0)
+        silu_pos(1)
         cast_w13(0,1)
-        quant_w13(0,1)
-        cast_w13(0,2)
-        load_w2(2,1)
-        load_w2(2,2)
-        quant_w13(0,2)
-        cast_g(1,0)
-        gather(1,1)
-        times(1,0)
-        times(1,1)
-        quant_da(1)
-        second_product(0,0)
-        second_product(0,1)
-        second_product(0,2)
-        cast_w2(2,0,'V')
-        load_w2(3,0)
-        quant_g(1,0)
-        cast_g(1,1)
+        first(1,1)
         gather(1,2)
-        cast_w13(1,0)
-        quant_w13(1,0)
-        cast_w13(1,1)
-        quant_w13(1,1)
-        cast_w13(1,2)
+        cast_w13(0,2)
+        load_w2(2,2)
+        load_w2(3,0)
+        load_a3(1)
         load_w2(3,1)
         load_w2(3,2)
-        quant_w13(1,2)
+        cast_w2(2,0)
         cast_w2(2,1)
-        quant_g(1,1)
-        cast_w2(2,2)
         load_w13(2)
-        cast_g(1,2)
-        second_product(1,0)
-        second_product(1,1)
-        second_product(1,2)
-        silu_pos(1)
-        slope2(1)
+        quant_g(1,1)
         quant_w2(2,0)
+        cast_w2(2,2)
+        slope1(1)
+        cast_g(1,2)
+        times(1,0)
+        times(1,1)
+        quant_da(0)
         quant_w2(2,1)
-        quant_w2(2,2)
         quant_g(1,2)
+        quant_w2(2,2)
         first(2,0)
+        quant_w13(0,1)
         first(2,1)
-        cast_w2(3,0,'V')
-        cast_w2(3,1)
+        cast_w2(3,0)
         load_w13(3)
+        cast_w2(3,1)
         cast_w2(3,2)
-        times(2,0)
-        times(2,1)
-        quant_da(2)
+        cast_w13(1,0)
+        quant_da(1)
+        slope2(1)
+        quant_w13(0,2)
         quant_w2(3,0)
         quant_w2(3,1)
+        times(2,0)
+        second(0,0)
+        second(0,1)
         quant_w2(3,2)
+        times(2,1)
+        quant_w13(1,0)
         first(3,0)
+        cast_w13(1,1)
         first(3,1)
-        cast_w13(2,0)
-        cast_w13(3,0)
-        quant_w13(2,0)
-        quant_w13(3,0)
+        quant_da(2)
         times(3,0)
         times(3,1)
+        second(0,2)
+        cast_w13(1,2,'SSSV')
         quant_da(3)
-        cast_w13(2,1)
-        cast_w13(3,1)
-        second_product(2,0)
-        second_product(3,0)
-        quant_w13(2,1)
-        quant_w13(3,1)
-        cast_w13(2,2)
-        cast_w13(3,2)
-        combine(0)
-        second_product(2,1)
-        second_product(3,1)
-        quant_w13(2,2)
-        quant_w13(3,2)
-        second_product(2,2)
-        second_product(3,2)
-        combine(1)
+        second(1,0)
+        quant_w13(1,1)
+        quant_w13(1,2)
+        second(1,1)
+        combine(0,'G')
+        second(1,2)
+        combine(1,'G')
         combine(2)

@@ -22,7 +22,7 @@ PAIR = 2 * C
 FILL = 32
 PASSES = N // 512
 MT = K // P
-G4B, W2B, W2Q, RAW = 3, 3, 4, 6
+G4B, W2B, W2Q, RAW = 3, 3, 5, 6
 
 FLOPS = 2 * S * H * N + 2 * 2 * S * H * K
 BYTES = 4 * (N * T + 2 * H * S + E * N * H + 2 * E * H * K + S + K * T) + 2 * 128 * (64 + 32 + 32)
@@ -246,135 +246,135 @@ def tile_moe_bdx_glu_silu_kernel(
             nc.sync.dma_start(out=out[m * P : (m + 1) * P, :], in_=both[:, 0, :])
 
         nc.sync.dma_start(offs_sb[:], offs)
-        load_dy(0,0)
         load_gate(0)
+        load_dy(0,0)
         load_dy(0,1)
-        load_pos()
-        load_a1(0)
         load_dy(0,2)
         load_dy(0,3)
         load_dy(1,0)
-        load_a1(1)
         load_dy(1,1)
         load_dy(1,2)
+        load_a1(0)
         load_w2(0,0)
         load_dy(1,3)
         load_dy(2,0)
         load_dy(2,1)
+        load_pos()
         load_dy(2,2)
-        load_w2(0,1)
         load_dy(2,3)
-        load_a1(2)
-        load_a1(3)
+        load_w2(0,1)
         load_gate(1)
         load_w2(0,2)
+        load_a1(1)
         load_w2(1,0)
         load_w2(1,1)
+        load_a1(2)
         load_w2(1,2)
+        load_a1(3)
         gather(0,0)
         sigmoid(0)
         gather(0,1)
-        sigmoid(1)
         cast_g(0,0)
-        quant_g(0,0)
         cast_w2(0,0)
-        cast_g(0,1)
-        cast_w2(0,1)
-        load_w13(0)
-        load_a3(0)
-        sigmoid(2)
-        sigmoid(3)
-        gather(0,2)
-        cast_g(0,2)
-        quant_w2(0,0)
-        quant_w2(0,1)
-        gather(1,0)
-        cast_w2(0,2,'V')
-        gather(1,1)
-        quant_g(0,1)
-        silu_neg(0)
-        slope1(0)
-        quant_w2(0,2)
-        cast_w2(1,0)
-        load_w13(1)
-        silu_pos(0)
-        quant_g(0,2)
-        first(0,0)
-        first(0,1)
-        slope2(0)
-        cast_w2(1,1)
         load_w2(2,0)
-        cast_g(1,0)
-        cast_w2(1,2,'V')
+        cast_g(0,1)
+        gather(0,2)
+        cast_w2(0,1)
+        cast_w2(0,2)
+        load_w13(0)
+        quant_w2(0,0)
+        quant_g(0,0)
+        gather(1,0)
+        quant_w2(0,1)
+        sigmoid(1)
+        cast_w2(1,0)
+        gather(1,1)
+        quant_w2(0,2)
+        quant_g(0,1)
+        cast_g(0,2)
+        cast_w2(1,1)
+        load_w13(1)
+        load_a3(0)
+        cast_w2(1,2)
         load_w2(2,1)
-        cast_w13(0,0,'SSSV')
-        cast_g(1,1,'V')
-        times(0,0)
         quant_w2(1,0)
-        quant_w2(1,1)
-        times(0,1)
-        quant_w13(0,0)
-        quant_g(1,0)
-        silu_neg(1)
-        quant_w2(1,2)
-        first(1,0)
-        silu_pos(1)
-        cast_w13(0,1)
-        first(1,1)
+        quant_g(0,2)
+        cast_g(1,0,'V')
         gather(1,2)
-        cast_w13(0,2)
-        load_w2(2,2)
-        load_w2(3,0)
-        load_a3(1)
-        load_w2(3,1)
-        load_w2(3,2)
+        sigmoid(2)
+        first(0,0)
+        quant_g(1,0)
+        sigmoid(3)
+        cast_g(1,1,'V')
+        cast_w13(0,0,'SVVV')
+        cast_g(1,2,'V')
+        silu_neg(0)
+        cast_w13(0,1)
+        first(0,1)
         cast_w2(2,0)
+        load_w2(2,2)
+        quant_w2(1,1)
+        slope1(0)
+        silu_pos(0)
+        quant_w13(0,0)
+        quant_w2(1,2)
+        cast_w13(0,2)
+        load_w2(3,0)
+        load_w2(3,1)
+        first(1,0)
+        first(1,1)
+        slope2(0)
+        load_a3(1)
+        load_w2(3,2)
+        quant_w2(2,0)
         cast_w2(2,1)
         load_w13(2)
-        quant_g(1,1)
-        quant_w2(2,0)
         cast_w2(2,2)
-        slope1(1)
-        cast_g(1,2)
-        times(1,0)
-        times(1,1)
-        quant_da(0)
-        quant_w2(2,1)
-        quant_g(1,2)
-        quant_w2(2,2)
-        first(2,0)
-        quant_w13(0,1)
-        first(2,1)
+        times(0,0)
+        times(0,1)
         cast_w2(3,0)
         load_w13(3)
-        cast_w2(3,1)
-        cast_w2(3,2)
-        cast_w13(1,0)
+        silu_neg(1)
+        times(1,0)
+        quant_w2(2,1)
+        quant_da(0)
+        quant_g(1,1)
+        times(1,1)
+        quant_w2(2,2)
         quant_da(1)
-        slope2(1)
-        quant_w13(0,2)
+        cast_w2(3,1)
+        quant_w13(0,1)
+        cast_w2(3,2)
+        quant_g(1,2)
+        slope1(1)
         quant_w2(3,0)
+        silu_pos(1)
+        cast_w13(1,0)
+        quant_w13(0,2)
+        first(2,0)
+        first(2,1)
         quant_w2(3,1)
-        times(2,0)
-        second(0,0)
-        second(0,1)
+        slope2(1)
         quant_w2(3,2)
+        second(0,0)
+        times(2,0)
         times(2,1)
-        quant_w13(1,0)
-        first(3,0)
-        cast_w13(1,1)
-        first(3,1)
-        quant_da(2)
-        times(3,0)
-        times(3,1)
+        second(0,1)
         second(0,2)
+        first(3,0)
+        quant_w13(1,0)
+        cast_w13(1,1)
+        times(3,0)
+        first(3,1)
+        times(3,1)
+        quant_da(2)
         cast_w13(1,2,'SSSV')
         quant_da(3)
-        second(1,0)
         quant_w13(1,1)
-        quant_w13(1,2)
+        second(1,0)
         second(1,1)
+        quant_w13(1,2)
         combine(0,'G')
-        second(1,2)
         combine(1,'G')
+        second(1,2)
         combine(2)

@@ -18,14 +18,22 @@ SILU = mybir.ActivationFunctionType.Silu
 SIGMOID = mybir.ActivationFunctionType.Sigmoid
 
 P = 128
-PAIR = 2 * C
-FILL = 32
-PASSES = N // 512
+WORD = 4
+PASS = P * WORD
+PASSES = N // PASS
 MT = K // P
-G4B, W2B, W2Q, RAW = 3, 3, 5, 6
+PAIR = 2 * C
+OFFS = PAIR // 16
+FILL = 32
+
+RAW_RING = 6
+F32_RING = 3
+W2_CAST_RING = 3
+W2_CODE_RING = 5
+G_CODE_RING = 5
 
 FLOPS = 2 * S * H * N + 2 * 2 * S * H * K
-BYTES = 4 * (N * T + 2 * H * S + E * N * H + 2 * E * H * K + S + K * T) + 2 * 128 * (64 + 32 + 32)
+BYTES = 4 * (N * T + 2 * H * S + E * N * H + 2 * E * H * K + S + K * T) + 2 * P * (S + 2 * T) // 16
 
 
 def tile_moe_bdx_glu_silu_kernel(
@@ -43,338 +51,354 @@ def tile_moe_bdx_glu_silu_kernel(
         pos1_sb = lists.tile([P, T // 16], U16, name="pos1_sb")
         pos2_sb = lists.tile([P, T // 16], U16, name="pos2_sb")
 
-        dy_rows = dyT.rearrange("(c p j) w -> c p (j w)", p=P, j=4)
-        a1_rows = a1.rearrange("(q t) n -> q t n", t=4)
-        a3_rows = a3.rearrange("(q t) n -> q t n", t=4)
+        dy_rows = dyT.rearrange("(c p j) w -> c p (j w)", p=P, j=WORD)
+        a1_rows = a1.rearrange("(p t) n -> p t n", t=WORD)
+        a3_rows = a3.rearrange("(p t) n -> p t n", t=WORD)
 
-        dy, gates, a3s, g4s, gbs, w2b, w13b, zs, das, dhs = {}, {}, {}, {}, {}, {}, {}, {}, {}, {}
-        hid = held.tile([P, 4, S], F32, name="hid")
-        sig = held.tile([P, 4, S], F32, name="sig")
-        raw2, raw13, gq, w2q, w13q, daq = {}, {}, {}, {}, {}, {}
-        dxs = []
+        act = held.tile([P, WORD, S], F32, name="act")
+        slope = held.tile([P, WORD, S], F32, name="slope")
+        dx_rows = []
         for m in range(MT):
-            dxs.append(held.tile([P, S], F32, name=f"dx_rows{m}"))
+            dx_rows.append(held.tile([P, S], F32, name=f"dx_rows{m}"))
+
+        dy, gates, a3_pair, w2_raw, w13_raw = {}, {}, {}, {}, {}
+        g_f32, g_bf16, neg_silu, w2_bf16, w13_bf16, da_bf16, dh_bank = {}, {}, {}, {}, {}, {}, {}
+        g_codes, w2_codes, w13_codes, da_codes = {}, {}, {}, {}
+
+        def slots(r):
+            return slice(r * PAIR, (r + 1) * PAIR)
+
 
         def load_gate(r):
             gates[r] = held.tile([P, PAIR], F32, name=f"gate{r}")
-            nc.sync.dma_start(out=gates[r][:], in_=gate[0:P, r * PAIR : (r + 1) * PAIR])
+            nc.sync.dma_start(out=gates[r][:], in_=gate[0:P, slots(r)])
 
         def load_dy(c, j):
-            t = held.tile([P, T + FILL], F32, name=f"dy{c}_{j}")
-            dy[c, j] = t
-            if j < 3:
-                nc.sync.dma_start(out=t[:], in_=dy_rows[c, :, j * T : (j + 1) * T + FILL])
+            tokens = held.tile([P, T + FILL], F32, name=f"dy{c}_{j}")
+            dy[c, j] = tokens
+            if j < WORD - 1:
+                nc.sync.dma_start(out=tokens[:], in_=dy_rows[c, :, j * T : (j + 1) * T + FILL])
             else:
-                nc.sync.dma_start(out=t[:, 0:T], in_=dy_rows[c, :, j * T : (j + 1) * T])
-                nc.sync.dma_start(out=t[:, T : T + FILL], in_=dy_rows[c, :, 0:FILL])
+                nc.sync.dma_start(out=tokens[:, 0:T], in_=dy_rows[c, :, j * T : (j + 1) * T])
+                nc.sync.dma_start(out=tokens[:, T : T + FILL], in_=dy_rows[c, :, 0:FILL])
 
         def load_a1(t):
-            nc.sync.dma_start(out=hid[:, t, :], in_=a1_rows[:, t, :])
+            nc.sync.dma_start(out=act[:, t, :], in_=a1_rows[:, t, :])
 
         def load_a3(r):
-            a3s[r] = ring.tile([P, 4, PAIR], F32, name="a3_sb", bufs=1)
-            nc.sync.dma_start(out=a3s[r][:], in_=a3_rows[:, :, r * PAIR : (r + 1) * PAIR])
+            a3_pair[r] = ring.tile([P, WORD, PAIR], F32, name="a3_pair", bufs=1)
+            nc.sync.dma_start(out=a3_pair[r][:], in_=a3_rows[:, :, slots(r)])
 
         def load_w2(e, c):
-            raw2[e, c] = ring.tile([P, 4, H], F32, name="w_raw", bufs=RAW)
+            w2_raw[e, c] = ring.tile([P, WORD, H], F32, name="w_raw", bufs=RAW_RING)
             nc.sync.dma_start(
-                out=raw2[e, c][:],
-                in_=w2[e, c * 512 : (c + 1) * 512, :].rearrange("(p j) w -> p j w", j=4),
+                out=w2_raw[e, c][:],
+                in_=w2[e, c * PASS : (c + 1) * PASS, :].rearrange("(p j) w -> p j w", j=WORD),
             )
 
         def load_w13(e):
-            for k, w in ((0, w1), (1, w3)):
-                raw13[e, k] = ring.tile([P, 4, K], F32, name="w_raw", bufs=RAW)
+            for which, w in enumerate((w1, w3)):
+                raw = ring.tile([P, WORD, K], F32, name="w_raw", bufs=RAW_RING)
+                w13_raw[e, which] = raw
                 nc.sync.dma_start(
-                    out=raw13[e, k][:], in_=w[e, :, :].rearrange("(p j) w -> p j w", j=4)
+                    out=raw[:], in_=w[e, :, :].rearrange("(p t) w -> p t w", t=WORD)
                 )
 
-        def load_pos():
-            nc.sync.dma_start(pos1_sb[:], pos1)
-            nc.sync.dma_start(pos2_sb[:], pos2)
 
-        def half(r):
-            return slice(r * PAIR, (r + 1) * PAIR)
+        def cast(dst, src, on_vector):
+            if on_vector:
+                nc.vector.tensor_copy(out=dst, in_=src)
+            else:
+                nc.scalar.copy(out=dst, in_=src)
+
+        def interleave(dst, src, on_vector):
+            cast(
+                dst.rearrange("p (n x) t -> p n t x", x=4),
+                src.rearrange("p t (n x) -> p n t x", x=4),
+                on_vector,
+            )
+
+        def quantise(columns, in_, name, depth):
+            codes = ring.tile([P, columns], U32, name=name + "_codes", bufs=depth, align_bytes=64)
+            scales = ring.tile([P, columns], U8, name=name + "_scales", bufs=depth, align_bytes=64)
+            nc.vector.quantize_mx(out=codes[:].bitcast(FP8X4), scales=scales[:], in_=in_)
+            return codes, scales
 
         def sigmoid(t):
-            nc.scalar.activation(out=sig[:, t, :], in_=hid[:, t, :], func=SIGMOID)
+            nc.scalar.activation(out=slope[:, t, :], in_=act[:, t, :], func=SIGMOID)
 
-        def silu_neg(r):
-            zs[r] = ring.tile([P, 4, PAIR], F32, name="f32", bufs=G4B)
-            nc.scalar.activation(out=zs[r][:], in_=hid[:, :, half(r)], func=SILU, scale=-1.0)
-
-        def silu_pos(r):
-            nc.scalar.activation(out=hid[:, :, half(r)], in_=hid[:, :, half(r)], func=SILU)
-
-        def slope1(r):
-            nc.vector.scalar_tensor_tensor(
-                out=sig[:, :, half(r)], in0=zs[r][:], scalar=1.0, in1=sig[:, :, half(r)], op0=SUB, op1=MULT
+        def silu_of_minus(r):
+            neg_silu[r] = ring.tile([P, WORD, PAIR], F32, name="f32", bufs=F32_RING)
+            nc.scalar.activation(
+                out=neg_silu[r][:], in_=act[:, :, slots(r)], func=SILU, scale=-1.0
             )
 
-        def slope2(r):
+        def silu(r):
+            nc.scalar.activation(out=act[:, :, slots(r)], in_=act[:, :, slots(r)], func=SILU)
+
+        def minus_d_silu(r):
             nc.vector.scalar_tensor_tensor(
-                out=sig[:, :, half(r)], in0=sig[:, :, half(r)], scalar=-1.0, in1=a3s[r][:], op0=MULT, op1=MULT
+                out=slope[:, :, slots(r)],
+                in0=neg_silu[r][:],
+                scalar=1.0,
+                in1=slope[:, :, slots(r)],
+                op0=SUB,
+                op1=MULT,
             )
 
-        def gather(r, c):
-            g4 = ring.tile([P, 4, PAIR], F32, name="f32", bufs=G4B)
-            g4s[r, c] = g4
-            for j in range(4):
+        def times_a3(r):
+            nc.vector.scalar_tensor_tensor(
+                out=slope[:, :, slots(r)],
+                in0=slope[:, :, slots(r)],
+                scalar=-1.0,
+                in1=a3_pair[r][:],
+                op0=MULT,
+                op1=MULT,
+            )
+
+        def gather_g(r, c):
+            g_f32[r, c] = ring.tile([P, WORD, PAIR], F32, name="f32", bufs=F32_RING)
+            for j in range(WORD):
                 nc.vector.tensor_tensor(
-                    g4[:, j, :],
-                    dy[c, j][:].indirect(offs_sb[:, r * PAIR // 16 : (r + 1) * PAIR // 16]),
+                    g_f32[r, c][:, j, :],
+                    dy[c, j][:].indirect(offs_sb[:, r * OFFS : (r + 1) * OFFS]),
                     gates[r][:],
                     MULT,
                 )
 
-        def interleave(engine, dst, src):
-            dst = dst.rearrange("p (c i) t -> p c t i", i=4)
-            src = src.rearrange("p t (c i) -> p c t i", i=4)
-            if engine == "S":
-                nc.scalar.copy(out=dst, in_=src)
-            else:
-                nc.vector.tensor_copy(out=dst, in_=src)
+        def cast_g(r, c, on_vector=False):
+            g_bf16[r, c] = ring.tile([P, PAIR, WORD], BF16, name="g_bf16", align_bytes=64)
+            interleave(g_bf16[r, c][:], g_f32[r, c][:], on_vector)
 
-        def cast_g(r, c, engine="S"):
-            gb = ring.tile([P, PAIR, 4], BF16, name="gb", bufs=2, align_bytes=64)
-            gbs[r, c] = gb
-            interleave(engine, gb[:], g4s[r, c][:])
-
-        def quant_g(r, c):
-            q = ring.tile([P, PAIR], U32, name="gq", bufs=5, align_bytes=64)
-            s = ring.tile([P, PAIR], U8, name="gs", bufs=5, align_bytes=64)
-            nc.vector.quantize_mx(
-                out=q[:].bitcast(FP8X4), scales=s[:], in_=gbs[r, c][:].rearrange("p w j -> p (w j)")
+        def quantise_g(r, c):
+            g_codes[r, c] = quantise(
+                PAIR, g_bf16[r, c][:].rearrange("p n j -> p (n j)"), "g", G_CODE_RING
             )
-            gq[r, c] = (q, s)
 
-        def cast_w2(e, c, engine="S"):
-            wb = ring.tile([P, H * 4], BF16, name="w2b", bufs=W2B, align_bytes=64)
-            w2b[e, c] = wb
-            dst = wb[:].rearrange("p (t m j) -> p m j t", t=4, j=4)
-            src = raw2[e, c][:].rearrange("p j (m t) -> p m j t", t=4)
-            if engine == "S":
-                nc.scalar.copy(out=dst, in_=src)
-            else:
-                nc.vector.tensor_copy(out=dst, in_=src)
-
-        def quant_w2(e, c):
-            q = ring.tile([P, H], U32, name="w2q", bufs=W2Q, align_bytes=64)
-            s = ring.tile([P, H], U8, name="w2s", bufs=W2Q, align_bytes=64)
-            nc.vector.quantize_mx(out=q[:].bitcast(FP8X4), scales=s[:], in_=w2b[e, c][:])
-            w2q[e, c] = (q, s)
-
-        def cast_w13(r, m, engines="SSSS"):
-            wb = ring.tile([P, 4, P, 4], BF16, name="w13b", bufs=2, align_bytes=64)
-            w13b[r, m] = wb
-            for i in range(4):
-                interleave(engines[i], wb[:, i], raw13[2 * r + i // 2, i % 2][:, :, m * P : (m + 1) * P])
-
-        def quant_w13(r, m):
-            q = ring.tile([P, 4 * P], U32, name="w13q", bufs=3, align_bytes=64)
-            s = ring.tile([P, 4 * P], U8, name="w13s", bufs=3, align_bytes=64)
-            nc.vector.quantize_mx(
-                out=q[:].bitcast(FP8X4), scales=s[:], in_=w13b[r, m][:].rearrange("p k w j -> p (k w j)")
+        def cast_w2(e, c):
+            w2_bf16[e, c] = ring.tile(
+                [P, H * WORD], BF16, name="w2_bf16", bufs=W2_CAST_RING, align_bytes=64
             )
-            w13q[r, m] = (q, s)
+            cast(
+                w2_bf16[e, c][:].rearrange("p (t m j) -> p m j t", t=WORD, j=WORD),
+                w2_raw[e, c][:].rearrange("p j (m t) -> p m j t", t=WORD),
+                on_vector=False,
+            )
 
-        def first(e, half):
-            r = e // 2
-            if half == 0:
-                das[e] = ring.tile([P, 2, C, 4], BF16, name="da", bufs=2, align_bytes=64)
-            da = das[e]
-            dh = psum.tile([P, 4, P], F32, name="dh")
-            col = (e % 2) * C + half * P
-            for t in range(4):
+        def quantise_w2(e, c):
+            w2_codes[e, c] = quantise(H, w2_bf16[e, c][:], "w2", W2_CODE_RING)
+
+        def cast_w13(r, m, vector_share=()):
+            w13_bf16[r, m] = ring.tile([P, 4, P, WORD], BF16, name="w13_bf16", align_bytes=64)
+            for number in range(4):
+                raw = w13_raw[2 * r + number // 2, number % 2]
+                interleave(
+                    w13_bf16[r, m][:, number],
+                    raw[:, :, m * P : (m + 1) * P],
+                    number in vector_share,
+                )
+
+        def quantise_w13(r, m):
+            w13_codes[r, m] = quantise(
+                4 * P, w13_bf16[r, m][:].rearrange("p w n t -> p (w n t)"), "w13", 3
+            )
+
+        def first_product(e, part):
+            if part == 0:
+                da_bf16[e] = ring.tile([P, 2, C, WORD], BF16, name="da_bf16", align_bytes=64)
+            dh = psum.tile([P, WORD, P], F32, name="dh")
+            dh_bank[e, part] = dh
+            col = (e % 2) * C + part * P
+            for t in range(WORD):
                 for c in range(PASSES):
-                    wq, ws = w2q[e, c]
-                    q, s = gq[r, c]
+                    w_codes, w_scales = w2_codes[e, c]
+                    codes, scales = g_codes[e // 2, c]
                     nc.tensor.matmul_mx(
                         out=dh[:, t, :],
-                        lhsT=wq[:, t * P : (t + 1) * P].bitcast(FP8X4),
-                        lhsT_scale=ws[:, t * P : (t + 1) * P],
-                        rhs=q[:, col : col + P].bitcast(FP8X4),
-                        rhs_scale=s[:, col : col + P],
+                        lhsT=w_codes[:, t * P : (t + 1) * P].bitcast(FP8X4),
+                        lhsT_scale=w_scales[:, t * P : (t + 1) * P],
+                        rhs=codes[:, col : col + P].bitcast(FP8X4),
+                        rhs_scale=scales[:, col : col + P],
                         start=(c == 0),
                         stop=(c == PASSES - 1),
                     )
-            dhs[e, half] = dh
 
-        def times(e, half):
-            da, dh = das[e], dhs[e, half]
-            slot = e * C + half * P
-            for k, factor in ((0, sig), (1, hid)):
+        def multiply_da(e, part):
+            slot = e * C + part * P
+            for which, factor in enumerate((slope, act)):
                 nc.vector.tensor_tensor(
-                    da[:, k, half * P : (half + 1) * P].rearrange("p (c i) t -> p c t i", i=4),
-                    dh[:].rearrange("p t (c i) -> p c t i", i=4),
-                    factor[:, :, slot : slot + P].rearrange("p t (c i) -> p c t i", i=4),
+                    da_bf16[e][:, which, part * P : (part + 1) * P].rearrange(
+                        "p (n x) t -> p n t x", x=4
+                    ),
+                    dh_bank[e, part][:].rearrange("p t (n x) -> p n t x", x=4),
+                    factor[:, :, slot : slot + P].rearrange("p t (n x) -> p n t x", x=4),
                     MULT,
                 )
 
-        def quant_da(e):
-            q = ring.tile([P, 2 * C], U32, name="daq", bufs=3, align_bytes=64)
-            s = ring.tile([P, 2 * C], U8, name="das", bufs=3, align_bytes=64)
-            nc.vector.quantize_mx(
-                out=q[:].bitcast(FP8X4), scales=s[:], in_=das[e][:].rearrange("p k w j -> p (k w j)")
+        def quantise_da(e):
+            da_codes[e] = quantise(
+                2 * C, da_bf16[e][:].rearrange("p w n t -> p (w n t)"), "da", 3
             )
-            daq[e] = (q, s)
 
-        def second(r, m):
-            wq, ws = w13q[r, m]
+        def second_product(r, m):
+            w_codes, w_scales = w13_codes[r, m]
             dx = psum.tile([P, 2, C], F32, name="dx")
             for i in range(2):
-                q, s = daq[2 * r + i]
-                for k in range(2):
-                    w = slice((2 * i + k) * P, (2 * i + k + 1) * P)
+                codes, scales = da_codes[2 * r + i]
+                for which in range(2):
+                    cols = slice((2 * i + which) * P, (2 * i + which + 1) * P)
                     nc.tensor.matmul_mx(
                         out=dx[:, i, :],
-                        lhsT=wq[:, w].bitcast(FP8X4),
-                        lhsT_scale=ws[:, w],
-                        rhs=q[:, k * C : (k + 1) * C].bitcast(FP8X4),
-                        rhs_scale=s[:, k * C : (k + 1) * C],
-                        start=(k == 0),
-                        stop=(k == 1),
+                        lhsT=w_codes[:, cols].bitcast(FP8X4),
+                        lhsT_scale=w_scales[:, cols],
+                        rhs=codes[:, which * C : (which + 1) * C].bitcast(FP8X4),
+                        rhs_scale=scales[:, which * C : (which + 1) * C],
+                        start=(which == 0),
+                        stop=(which == 1),
                     )
-            nc.scalar.copy(out=dxs[m][:, half(r)], in_=dx[:].rearrange("p i n -> p (i n)"))
+            nc.scalar.copy(out=dx_rows[m][:, slots(r)], in_=dx[:].rearrange("p i n -> p (i n)"))
 
-        def combine(m, engine="V"):
-            both = ring.tile([P, 2, T], F32, name="f32", bufs=G4B)
-            nc.vector.tensor_copy(both[:, 0, :], dxs[m][:].indirect(pos1_sb[:]))
-            nc.vector.tensor_copy(both[:, 1, :], dxs[m][:].indirect(pos2_sb[:]))
-            adder = nc.vector if engine == "V" else nc.gpsimd
+        def combine(m, adder):
+            both = ring.tile([P, 2, T], F32, name="f32", bufs=F32_RING)
+            nc.vector.tensor_copy(both[:, 0, :], dx_rows[m][:].indirect(pos1_sb[:]))
+            nc.vector.tensor_copy(both[:, 1, :], dx_rows[m][:].indirect(pos2_sb[:]))
             adder.tensor_tensor(both[:, 0, :], both[:, 0, :], both[:, 1, :], ADD)
             nc.sync.dma_start(out=out[m * P : (m + 1) * P, :], in_=both[:, 0, :])
 
+
         nc.sync.dma_start(offs_sb[:], offs)
+        load_dy(0, 0)
         load_gate(0)
-        load_dy(0,0)
-        load_dy(0,1)
-        load_dy(0,2)
-        load_dy(0,3)
-        load_dy(1,0)
-        load_dy(1,1)
-        load_dy(1,2)
+        load_dy(0, 1)
+        load_dy(0, 2)
         load_a1(0)
-        load_w2(0,0)
-        load_dy(1,3)
-        load_dy(2,0)
-        load_dy(2,1)
-        load_pos()
-        load_dy(2,2)
-        load_dy(2,3)
-        load_w2(0,1)
-        load_gate(1)
-        load_w2(0,2)
         load_a1(1)
-        load_w2(1,0)
-        load_w2(1,1)
+        load_dy(0, 3)
+        load_dy(1, 0)
+        load_dy(1, 1)
         load_a1(2)
-        load_w2(1,2)
+        load_dy(1, 2)
+        load_w2(0, 0)
+        load_dy(1, 3)
+        load_dy(2, 0)
+        load_dy(2, 1)
+        load_w2(0, 1)
         load_a1(3)
-        gather(0,0)
+        load_dy(2, 2)
+        load_gate(1)
+        load_dy(2, 3)
+        load_w2(0, 2)
+        for c in range(PASSES):
+            load_w2(1, c)
+
+        gather_g(0, 0)
         sigmoid(0)
-        gather(0,1)
-        cast_g(0,0)
-        cast_w2(0,0)
-        load_w2(2,0)
-        cast_g(0,1)
-        gather(0,2)
-        cast_w2(0,1)
-        cast_w2(0,2)
-        load_w13(0)
-        quant_w2(0,0)
-        quant_g(0,0)
-        gather(1,0)
-        quant_w2(0,1)
         sigmoid(1)
-        cast_w2(1,0)
-        gather(1,1)
-        quant_w2(0,2)
-        quant_g(0,1)
-        cast_g(0,2)
-        cast_w2(1,1)
-        load_w13(1)
-        load_a3(0)
-        cast_w2(1,2)
-        load_w2(2,1)
-        quant_w2(1,0)
-        quant_g(0,2)
-        cast_g(1,0,'V')
-        gather(1,2)
+        gather_g(0, 1)
+        cast_g(0, 0)
         sigmoid(2)
-        first(0,0)
-        quant_g(1,0)
+        quantise_g(0, 0)
+        cast_w2(0, 0)
+        load_w2(2, 0)
+        nc.sync.dma_start(pos1_sb[:], pos1)
+        nc.sync.dma_start(pos2_sb[:], pos2)
+        load_a3(0)
+        cast_g(0, 1)
+        cast_w2(0, 1)
+        quantise_w2(0, 0)
+        gather_g(0, 2)
+        gather_g(1, 0)
         sigmoid(3)
-        cast_g(1,1,'V')
-        cast_w13(0,0,'SVVV')
-        cast_g(1,2,'V')
-        silu_neg(0)
-        cast_w13(0,1)
-        first(0,1)
-        cast_w2(2,0)
-        load_w2(2,2)
-        quant_w2(1,1)
-        slope1(0)
-        silu_pos(0)
-        quant_w13(0,0)
-        quant_w2(1,2)
-        cast_w13(0,2)
-        load_w2(3,0)
-        load_w2(3,1)
-        first(1,0)
-        first(1,1)
-        slope2(0)
+        silu_of_minus(0)
+        cast_w2(0, 2)
+        load_w13(0)
+        cast_g(0, 2)
+        quantise_w2(0, 1)
+        cast_w2(1, 0)
+        cast_w2(1, 1)
+        load_w13(1)
+        minus_d_silu(0)
+        quantise_g(0, 1)
+        quantise_w2(0, 2)
+        quantise_g(0, 2)
+
+        gather_g(1, 1)
+        quantise_w2(1, 0)
+        cast_w2(1, 2)
+        load_w2(2, 1)
+        times_a3(0)
+        first_product(0, 0)
+        cast_g(1, 0)
+        cast_w13(0, 0, vector_share=(1, 3))
+        quantise_w2(1, 1)
+        gather_g(1, 2)
+        first_product(0, 1)
+        quantise_w13(0, 0)
+        cast_w2(2, 0)
+        load_w2(2, 2)
         load_a3(1)
-        load_w2(3,2)
-        quant_w2(2,0)
-        cast_w2(2,1)
+        quantise_w2(1, 2)
+        first_product(1, 0)
+        silu(0)
+        cast_w13(0, 1)
+        quantise_w2(2, 0)
+        multiply_da(0, 0)
+        quantise_g(1, 0)
+        cast_g(1, 1)
+        cast_w2(2, 1)
+        cast_w13(0, 2)
+        for c in range(PASSES):
+            load_w2(3, c)
         load_w13(2)
-        cast_w2(2,2)
-        times(0,0)
-        times(0,1)
-        cast_w2(3,0)
+        cast_w2(2, 2)
+        quantise_w2(2, 1)
+        first_product(1, 1)
+        multiply_da(0, 1)
+        quantise_w13(0, 1)
+        quantise_w13(0, 2)
+        multiply_da(1, 0)
+        cast_g(1, 2, on_vector=True)
+        silu_of_minus(1)
+        cast_w2(3, 0)
         load_w13(3)
-        silu_neg(1)
-        times(1,0)
-        quant_w2(2,1)
-        quant_da(0)
-        quant_g(1,1)
-        times(1,1)
-        quant_w2(2,2)
-        quant_da(1)
-        cast_w2(3,1)
-        quant_w13(0,1)
-        cast_w2(3,2)
-        quant_g(1,2)
-        slope1(1)
-        quant_w2(3,0)
-        silu_pos(1)
-        cast_w13(1,0)
-        quant_w13(0,2)
-        first(2,0)
-        first(2,1)
-        quant_w2(3,1)
-        slope2(1)
-        quant_w2(3,2)
-        second(0,0)
-        times(2,0)
-        times(2,1)
-        second(0,1)
-        second(0,2)
-        first(3,0)
-        quant_w13(1,0)
-        cast_w13(1,1)
-        times(3,0)
-        first(3,1)
-        times(3,1)
-        quant_da(2)
-        cast_w13(1,2,'SSSV')
-        quant_da(3)
-        quant_w13(1,1)
-        second(1,0)
-        second(1,1)
-        quant_w13(1,2)
-        combine(0,'G')
-        combine(1,'G')
-        second(1,2)
-        combine(2)
+        quantise_w2(2, 2)
+        quantise_g(1, 1)
+        quantise_da(0)
+        multiply_da(1, 1)
+        quantise_g(1, 2)
+        minus_d_silu(1)
+        quantise_w2(3, 0)
+        cast_w2(3, 1)
+        cast_w2(3, 2)
+        quantise_da(1)
+        silu(1)
+
+        first_product(2, 0)
+        quantise_w2(3, 1)
+        cast_w13(1, 0)
+        first_product(2, 1)
+        second_product(0, 0)
+        cast_w13(1, 1)
+        times_a3(1)
+        quantise_w2(3, 2)
+        first_product(3, 0)
+        multiply_da(2, 0)
+        multiply_da(2, 1)
+        quantise_w13(1, 0)
+        cast_w13(1, 2)
+        first_product(3, 1)
+        quantise_da(2)
+        multiply_da(3, 0)
+        multiply_da(3, 1)
+        second_product(0, 1)
+        second_product(0, 2)
+        quantise_da(3)
+
+        second_product(1, 0)
+        quantise_w13(1, 1)
+        second_product(1, 1)
+        quantise_w13(1, 2)
+        combine(0, nc.gpsimd)
+        combine(1, nc.gpsimd)
+        second_product(1, 2)
+        combine(2, nc.vector)

from contextlib import ExitStack

import concourse.mybir as mybir

N, T, E, C, H, K = 1536, 512, 4, 256, 512, 384
S = E * C

F32 = mybir.dt.float32
BF16 = mybir.dt.bfloat16
U32 = mybir.dt.uint32
U16 = mybir.dt.uint16
U8 = mybir.dt.uint8
FP8X4 = mybir.dt.float8_e4m3fn_x4
MULT = mybir.AluOpType.mult
ADD = mybir.AluOpType.add
SUB = mybir.AluOpType.subtract
SILU = mybir.ActivationFunctionType.Silu
SIGMOID = mybir.ActivationFunctionType.Sigmoid

P = 128
WORD = 4
PASS = P * WORD
PASSES = N // PASS
MT = K // P
PAIR = 2 * C
OFFS = PAIR // 16
FILL = 32

RAW_RING = 6
F32_RING = 3
W2_CAST_RING = 3
W2_CODE_RING = 5
G_CODE_RING = 5

FLOPS = 2 * S * H * N + 2 * 2 * S * H * K
BYTES = 4 * (N * T + 2 * H * S + E * N * H + 2 * E * H * K + S + K * T) + 2 * P * (S + 2 * T) // 16


def tile_moe_bdx_glu_silu_kernel(
    tc, dyT, a1, a3, w2, w1, w3, gate, offs, pos1, pos2, out
):
    nc = tc.nc

    with ExitStack() as ctx:
        lists = ctx.enter_context(tc.tile_pool(name="lists", bufs=1))
        held = ctx.enter_context(tc.tile_pool(name="held", bufs=1))
        ring = ctx.enter_context(tc.tile_pool(name="ring", bufs=2))
        psum = ctx.enter_context(tc.psum_pool(name="psum", bufs=4))

        offs_sb = lists.tile([P, S // 16], U16, name="offs_sb")
        pos1_sb = lists.tile([P, T // 16], U16, name="pos1_sb")
        pos2_sb = lists.tile([P, T // 16], U16, name="pos2_sb")

        dy_rows = dyT.rearrange("(c p j) w -> c p (j w)", p=P, j=WORD)
        a1_rows = a1.rearrange("(p t) n -> p t n", t=WORD)
        a3_rows = a3.rearrange("(p t) n -> p t n", t=WORD)

        act = held.tile([P, WORD, S], F32, name="act")
        slope = held.tile([P, WORD, S], F32, name="slope")
        dx_rows = []
        for m in range(MT):
            dx_rows.append(held.tile([P, S], F32, name=f"dx_rows{m}"))

        dy, gates, a3_pair, w2_raw, w13_raw = {}, {}, {}, {}, {}
        g_f32, g_bf16, neg_silu, w2_bf16, w13_bf16, da_bf16, dh_bank = {}, {}, {}, {}, {}, {}, {}
        g_codes, w2_codes, w13_codes, da_codes = {}, {}, {}, {}

        def slots(r):
            return slice(r * PAIR, (r + 1) * PAIR)


        def load_gate(r):
            gates[r] = held.tile([P, PAIR], F32, name=f"gate{r}")
            nc.sync.dma_start(out=gates[r][:], in_=gate[0:P, slots(r)])

        def load_dy(c, j):
            tokens = held.tile([P, T + FILL], F32, name=f"dy{c}_{j}")
            dy[c, j] = tokens
            if j < WORD - 1:
                nc.sync.dma_start(out=tokens[:], in_=dy_rows[c, :, j * T : (j + 1) * T + FILL])
            else:
                nc.sync.dma_start(out=tokens[:, 0:T], in_=dy_rows[c, :, j * T : (j + 1) * T])
                nc.sync.dma_start(out=tokens[:, T : T + FILL], in_=dy_rows[c, :, 0:FILL])

        def load_a1(t):
            nc.sync.dma_start(out=act[:, t, :], in_=a1_rows[:, t, :])

        def load_a3(r):
            a3_pair[r] = ring.tile([P, WORD, PAIR], F32, name="a3_pair", bufs=1)
            nc.sync.dma_start(out=a3_pair[r][:], in_=a3_rows[:, :, slots(r)])

        def load_w2(e, c):
            w2_raw[e, c] = ring.tile([P, WORD, H], F32, name="w_raw", bufs=RAW_RING)
            nc.sync.dma_start(
                out=w2_raw[e, c][:],
                in_=w2[e, c * PASS : (c + 1) * PASS, :].rearrange("(p j) w -> p j w", j=WORD),
            )

        def load_w13(e):
            for which, w in enumerate((w1, w3)):
                raw = ring.tile([P, WORD, K], F32, name="w_raw", bufs=RAW_RING)
                w13_raw[e, which] = raw
                nc.sync.dma_start(
                    out=raw[:], in_=w[e, :, :].rearrange("(p t) w -> p t w", t=WORD)
                )


        def cast(dst, src, on_vector):
            if on_vector:
                nc.vector.tensor_copy(out=dst, in_=src)
            else:
                nc.scalar.copy(out=dst, in_=src)

        def interleave(dst, src, on_vector):
            cast(
                dst.rearrange("p (n x) t -> p n t x", x=4),
                src.rearrange("p t (n x) -> p n t x", x=4),
                on_vector,
            )

        def quantise(columns, in_, name, depth):
            codes = ring.tile([P, columns], U32, name=name + "_codes", bufs=depth, align_bytes=64)
            scales = ring.tile([P, columns], U8, name=name + "_scales", bufs=depth, align_bytes=64)
            nc.vector.quantize_mx(out=codes[:].bitcast(FP8X4), scales=scales[:], in_=in_)
            return codes, scales

        def sigmoid(t):
            nc.scalar.activation(out=slope[:, t, :], in_=act[:, t, :], func=SIGMOID)

        def silu_of_minus(r):
            neg_silu[r] = ring.tile([P, WORD, PAIR], F32, name="f32", bufs=F32_RING)
            nc.scalar.activation(
                out=neg_silu[r][:], in_=act[:, :, slots(r)], func=SILU, scale=-1.0
            )

        def silu(r):
            nc.scalar.activation(out=act[:, :, slots(r)], in_=act[:, :, slots(r)], func=SILU)

        def minus_d_silu(r):
            nc.vector.scalar_tensor_tensor(
                out=slope[:, :, slots(r)],
                in0=neg_silu[r][:],
                scalar=1.0,
                in1=slope[:, :, slots(r)],
                op0=SUB,
                op1=MULT,
            )

        def times_a3(r):
            nc.vector.scalar_tensor_tensor(
                out=slope[:, :, slots(r)],
                in0=slope[:, :, slots(r)],
                scalar=-1.0,
                in1=a3_pair[r][:],
                op0=MULT,
                op1=MULT,
            )

        def gather_g(r, c):
            g_f32[r, c] = ring.tile([P, WORD, PAIR], F32, name="f32", bufs=F32_RING)
            for j in range(WORD):
                nc.vector.tensor_tensor(
                    g_f32[r, c][:, j, :],
                    dy[c, j][:].indirect(offs_sb[:, r * OFFS : (r + 1) * OFFS]),
                    gates[r][:],
                    MULT,
                )

        def cast_g(r, c, on_vector=False):
            g_bf16[r, c] = ring.tile([P, PAIR, WORD], BF16, name="g_bf16", align_bytes=64)
            interleave(g_bf16[r, c][:], g_f32[r, c][:], on_vector)

        def quantise_g(r, c):
            g_codes[r, c] = quantise(
                PAIR, g_bf16[r, c][:].rearrange("p n j -> p (n j)"), "g", G_CODE_RING
            )

        def cast_w2(e, c):
            w2_bf16[e, c] = ring.tile(
                [P, H * WORD], BF16, name="w2_bf16", bufs=W2_CAST_RING, align_bytes=64
            )
            cast(
                w2_bf16[e, c][:].rearrange("p (t m j) -> p m j t", t=WORD, j=WORD),
                w2_raw[e, c][:].rearrange("p j (m t) -> p m j t", t=WORD),
                on_vector=False,
            )

        def quantise_w2(e, c):
            w2_codes[e, c] = quantise(H, w2_bf16[e, c][:], "w2", W2_CODE_RING)

        def cast_w13(r, m, vector_share=()):
            w13_bf16[r, m] = ring.tile([P, 4, P, WORD], BF16, name="w13_bf16", align_bytes=64)
            for number in range(4):
                raw = w13_raw[2 * r + number // 2, number % 2]
                interleave(
                    w13_bf16[r, m][:, number],
                    raw[:, :, m * P : (m + 1) * P],
                    number in vector_share,
                )

        def quantise_w13(r, m):
            w13_codes[r, m] = quantise(
                4 * P, w13_bf16[r, m][:].rearrange("p w n t -> p (w n t)"), "w13", 3
            )

        def first_product(e, part):
            if part == 0:
                da_bf16[e] = ring.tile([P, 2, C, WORD], BF16, name="da_bf16", align_bytes=64)
            dh = psum.tile([P, WORD, P], F32, name="dh")
            dh_bank[e, part] = dh
            col = (e % 2) * C + part * P
            for t in range(WORD):
                for c in range(PASSES):
                    w_codes, w_scales = w2_codes[e, c]
                    codes, scales = g_codes[e // 2, c]
                    nc.tensor.matmul_mx(
                        out=dh[:, t, :],
                        lhsT=w_codes[:, t * P : (t + 1) * P].bitcast(FP8X4),
                        lhsT_scale=w_scales[:, t * P : (t + 1) * P],
                        rhs=codes[:, col : col + P].bitcast(FP8X4),
                        rhs_scale=scales[:, col : col + P],
                        start=(c == 0),
                        stop=(c == PASSES - 1),
                    )

        def multiply_da(e, part):
            slot = e * C + part * P
            for which, factor in enumerate((slope, act)):
                nc.vector.tensor_tensor(
                    da_bf16[e][:, which, part * P : (part + 1) * P].rearrange(
                        "p (n x) t -> p n t x", x=4
                    ),
                    dh_bank[e, part][:].rearrange("p t (n x) -> p n t x", x=4),
                    factor[:, :, slot : slot + P].rearrange("p t (n x) -> p n t x", x=4),
                    MULT,
                )

        def quantise_da(e):
            da_codes[e] = quantise(
                2 * C, da_bf16[e][:].rearrange("p w n t -> p (w n t)"), "da", 3
            )

        def second_product(r, m):
            w_codes, w_scales = w13_codes[r, m]
            dx = psum.tile([P, 2, C], F32, name="dx")
            for i in range(2):
                codes, scales = da_codes[2 * r + i]
                for which in range(2):
                    cols = slice((2 * i + which) * P, (2 * i + which + 1) * P)
                    nc.tensor.matmul_mx(
                        out=dx[:, i, :],
                        lhsT=w_codes[:, cols].bitcast(FP8X4),
                        lhsT_scale=w_scales[:, cols],
                        rhs=codes[:, which * C : (which + 1) * C].bitcast(FP8X4),
                        rhs_scale=scales[:, which * C : (which + 1) * C],
                        start=(which == 0),
                        stop=(which == 1),
                    )
            nc.scalar.copy(out=dx_rows[m][:, slots(r)], in_=dx[:].rearrange("p i n -> p (i n)"))

        def combine(m, adder):
            both = ring.tile([P, 2, T], F32, name="f32", bufs=F32_RING)
            nc.vector.tensor_copy(both[:, 0, :], dx_rows[m][:].indirect(pos1_sb[:]))
            nc.vector.tensor_copy(both[:, 1, :], dx_rows[m][:].indirect(pos2_sb[:]))
            adder.tensor_tensor(both[:, 0, :], both[:, 0, :], both[:, 1, :], ADD)
            nc.sync.dma_start(out=out[m * P : (m + 1) * P, :], in_=both[:, 0, :])


        nc.sync.dma_start(offs_sb[:], offs)
        load_dy(0, 0)
        load_gate(0)
        load_dy(0, 1)
        load_dy(0, 2)
        load_a1(0)
        load_a1(1)
        load_dy(0, 3)
        load_dy(1, 0)
        load_dy(1, 1)
        load_a1(2)
        load_dy(1, 2)
        load_w2(0, 0)
        load_dy(1, 3)
        load_dy(2, 0)
        load_dy(2, 1)
        load_w2(0, 1)
        load_a1(3)
        load_dy(2, 2)
        load_gate(1)
        load_dy(2, 3)
        load_w2(0, 2)
        for c in range(PASSES):
            load_w2(1, c)

        gather_g(0, 0)
        sigmoid(0)
        sigmoid(1)
        gather_g(0, 1)
        cast_g(0, 0)
        sigmoid(2)
        quantise_g(0, 0)
        cast_w2(0, 0)
        load_w2(2, 0)
        nc.sync.dma_start(pos1_sb[:], pos1)
        nc.sync.dma_start(pos2_sb[:], pos2)
        load_a3(0)
        cast_g(0, 1)
        cast_w2(0, 1)
        quantise_w2(0, 0)
        gather_g(0, 2)
        gather_g(1, 0)
        sigmoid(3)
        silu_of_minus(0)
        cast_w2(0, 2)
        load_w13(0)
        cast_g(0, 2)
        quantise_w2(0, 1)
        cast_w2(1, 0)
        cast_w2(1, 1)
        load_w13(1)
        minus_d_silu(0)
        quantise_g(0, 1)
        quantise_w2(0, 2)
        quantise_g(0, 2)

        gather_g(1, 1)
        quantise_w2(1, 0)
        cast_w2(1, 2)
        load_w2(2, 1)
        times_a3(0)
        first_product(0, 0)
        cast_g(1, 0)
        cast_w13(0, 0, vector_share=(1, 3))
        quantise_w2(1, 1)
        gather_g(1, 2)
        first_product(0, 1)
        quantise_w13(0, 0)
        cast_w2(2, 0)
        load_w2(2, 2)
        load_a3(1)
        quantise_w2(1, 2)
        first_product(1, 0)
        silu(0)
        cast_w13(0, 1)
        quantise_w2(2, 0)
        multiply_da(0, 0)
        quantise_g(1, 0)
        cast_g(1, 1)
        cast_w2(2, 1)
        cast_w13(0, 2)
        for c in range(PASSES):
            load_w2(3, c)
        load_w13(2)
        cast_w2(2, 2)
        quantise_w2(2, 1)
        first_product(1, 1)
        multiply_da(0, 1)
        quantise_w13(0, 1)
        quantise_w13(0, 2)
        multiply_da(1, 0)
        cast_g(1, 2, on_vector=True)
        silu_of_minus(1)
        cast_w2(3, 0)
        load_w13(3)
        quantise_w2(2, 2)
        quantise_g(1, 1)
        quantise_da(0)
        multiply_da(1, 1)
        quantise_g(1, 2)
        minus_d_silu(1)
        quantise_w2(3, 0)
        cast_w2(3, 1)
        cast_w2(3, 2)
        quantise_da(1)
        silu(1)

        first_product(2, 0)
        quantise_w2(3, 1)
        cast_w13(1, 0)
        first_product(2, 1)
        second_product(0, 0)
        cast_w13(1, 1)
        times_a3(1)
        quantise_w2(3, 2)
        first_product(3, 0)
        multiply_da(2, 0)
        multiply_da(2, 1)
        quantise_w13(1, 0)
        cast_w13(1, 2)
        first_product(3, 1)
        quantise_da(2)
        multiply_da(3, 0)
        multiply_da(3, 1)
        second_product(0, 1)
        second_product(0, 2)
        quantise_da(3)

        second_product(1, 0)
        quantise_w13(1, 1)
        second_product(1, 1)
        quantise_w13(1, 2)
        combine(0, nc.gpsimd)
        combine(1, nc.gpsimd)
        second_product(1, 2)
        combine(2, nc.vector)
